import numpy as np
import ml_dtypes


def mxq(x, axis, fmt="e4m3"):
    dtype, down = {"e4m3": (ml_dtypes.float8_e4m3fn, 7), "e5m2": (ml_dtypes.float8_e5m2, 14)}[fmt]
    v = np.moveaxis(np.asarray(x, np.float32).astype(ml_dtypes.bfloat16).astype(np.float64), axis, -1)
    blocks = v.reshape(v.shape[:-1] + (-1, 32))
    amax = np.abs(blocks).max(-1, keepdims=True)
    byte = np.maximum(np.where(amax > 0, np.frexp(amax)[1] - 1 + 127, 0) - down, 1)
    scale = np.exp2(byte - 127.0)
    codes = (blocks / scale).astype(np.float32).astype(dtype).astype(np.float64)
    return np.moveaxis((codes * scale).reshape(v.shape), -1, axis)


WIDE = False


def mx_kscale(k):
    if not WIDE:
        return np.ones(k)
    levels = np.array([10, -10, 5, -5, 0])
    if k % 512:
        return np.exp2(np.random.permutation(np.resize(levels, k // 32))).repeat(32)
    a = np.empty((k // 512, 16))
    for p in range(k // 512):
        a[p, :8] = np.random.permutation(np.resize(levels, 8))
        for g in range(8):
            far = levels[np.abs(levels - a[p, g]) >= 10]
            a[p, g + 8] = far[np.random.randint(len(far))]
    return np.exp2(a.ravel()).repeat(32)


BF16 = ml_dtypes.bfloat16


def bf(x):
    return np.asarray(x, np.float32).astype(BF16)


def f64(x):
    return np.asarray(x).astype(np.float64)


B, S, D = 2, 512, 512
TWO = 2


def softmax_last(logit):
    top = np.max(logit, axis=-1, keepdims=True)
    e = np.exp(logit - top)
    return e / np.sum(e, axis=-1, keepdims=True)


def draw0():
    s, t = mx_kscale(D), mx_kscale(S)
    x = bf(np.random.standard_normal((B, S, D)) * s)
    w = bf(np.random.standard_normal((D, S)) * (2.0 / np.sqrt(D)) / s[:, None])
    rnd = bf(np.random.standard_normal((S, S)) * 1.5)
    mix = bf(np.random.uniform(0.5, 0.9, (TWO,)))
    wv = bf(np.random.standard_normal((D, D)) / np.sqrt(D) / s[:, None])
    c = bf(np.random.standard_normal(S) * (0.25 * np.sqrt(S)) * t)
    u = bf((1.0 + 0.1 * np.random.standard_normal(S)) / t)
    return {"x": x, "w": w, "rnd": rnd, "mix": mix, "wv": wv, "c": c, "u": u}


def core(x, w, rnd, mix, wv, c, u):
    mix = f64(mix)
    xq = mxq(f64(x), 2, "e4m3")
    syn = xq @ mxq(f64(w), 0, "e4m3")
    logit = mix[0] * syn + mix[1] * f64(rnd)[None, :, :]
    p = softmax_last(logit)
    pc = p * f64(c)[None, None, :]
    v = f64(u)[None, :, None] * (xq @ mxq(f64(wv), 0, "e4m3"))
    return mxq(pc, 2, "e4m3") @ mxq(v, 1, "e4m3")


def e4m3fn_bytes(y):
    return np.clip(np.asarray(y, np.float64), -448.0, 448.0).astype(np.float32).astype(ml_dtypes.float8_e4m3fn).view(np.uint8)


def e4m3fn_values(b):
    return np.asarray(b, np.uint8).view(ml_dtypes.float8_e4m3fn).astype(np.float64)


def setup_inputs():
    d = draw0()
    x0 = np.asarray(d['x']).astype(np.float64)
    s = (np.max(np.abs(x0), axis=(0, 1), keepdims=True) / 448.0).astype(np.float32)
    out = {}
    for k, v in d.items():
        if k == 'x':
            out['x_bytes'] = e4m3fn_bytes(x0 / s.astype(np.float64))
            out['x_scale'] = s
        else:
            out[k] = v
    return out


def reference(x_bytes, x_scale, w, rnd, mix, wv, c, u):
    return core(e4m3fn_values(x_bytes) * x_scale.astype(np.float64), w, rnd, mix, wv, c, u)

from contextlib import ExitStack

import concourse.mybir as mybir
from concourse.masks import make_identity

B, S, D = 2, 512, 512
FLOPS = 3 * 2 * B * S * S * D

F32 = mybir.dt.float32
BF16 = mybir.dt.bfloat16
U32 = mybir.dt.uint32
U8 = mybir.dt.uint8
FP8 = mybir.dt.float8_e4m3fn
FP8X4 = mybir.dt.float8_e4m3fn_x4
ADD = mybir.AluOpType.add
MULT = mybir.AluOpType.mult
MIN = mybir.AluOpType.min
ACT = mybir.ActivationFunctionType
AX = mybir.AxisListType

P = 128
T = 4
H = 256
BANK = 512

ORDER = """
    weave_w turn_scale spread_scale widen widen weave_w widen widen turn_x turn_x add_rnd unload_x widen widen
    widen widen weave_wv unload_x quantise_w turn_x turn_x add_rnd quantise_x weave_wv score quantise_wv score
    value unload_x unload_x value unload_score score quantise_x unload_score unload_value value score
    unload_value value unload_value unload_value unload_score unload_score value score add_score reorder_c
    unload_value add_score score value row_max unload_score row_max exp exp quantise_value score score
    unload_value reciprocal unload_score add_rnd add_score row_max add_rnd add_score probs turn_probs
    unload_score value exp row_max add_rnd unload_score probs exp add_score unload_value reciprocal turn_probs
    row_max unload_probs add_rnd add_score unload_probs quantise_probs row_max exp exp probs result add_rnd
    add_score store probs reciprocal row_max turn_probs add_rnd unload_probs turn_probs add_score unload_probs
    probs row_max result exp quantise_probs value store exp turn_probs result probs unload_value unload_probs
    turn_probs store reciprocal quantise_probs unload_probs result quantise_value probs quantise_probs result
    store store turn_probs result probs unload_probs quantise_probs turn_probs result unload_probs store
    quantise_probs result store store result store
"""


def tile_mixturedenserandomsynthesizer_kernel(tc, x_bytes, x_scale, w, rnd, mix, wv, c, u, out):
    nc = tc.nc
    with ExitStack() as ctx:
        keep = ctx.enter_context(tc.tile_pool(name="keep", bufs=1))
        stage_out = ctx.enter_context(tc.tile_pool(name="stage_out", bufs=B * T))
        ps_turn = ctx.enter_context(tc.psum_pool(name="ps_turn", bufs=2))
        ps_mx = ctx.enter_context(tc.psum_pool(name="ps_mx", bufs=4))
        ps_logit = ctx.enter_context(tc.psum_pool(name="ps_logit", bufs=2))
        ctx.enter_context(tc.manual_schedule())

        def sbuf(name, shape, dtype):
            return keep.tile(shape, dtype, name=name, align_bytes=64)

        def per_batch(name, shape, dtype):
            return [sbuf("%s%d" % (name, b), shape, dtype) for b in range(B)]

        def per_tile(name, shape, dtype):
            return [[sbuf("%s%d%d" % (name, b, t), shape, dtype) for t in range(T)] for b in range(B)]

        def blk(t):
            return slice(t * P, (t + 1) * P)

        mix_bc = sbuf("mix_bc", [P, 2], BF16)
        u4 = sbuf("u4", [P, T], BF16)
        scale4 = sbuf("scale4", [P, T], F32)
        x_raw = per_batch("x_raw", [P, T, D], U8)
        w_raw = [sbuf("w_raw%d" % h, [P, T, H], BF16) for h in range(2)]
        wv_raw = [sbuf("wv_raw%d" % h, [P, T, H], BF16) for h in range(2)]
        rnd_sb = sbuf("rnd_sb", [P, T, S], BF16)
        c_bc = sbuf("c_bc", [P, S], BF16)
        c_split = sbuf("c_split", [P, S], BF16)
        warm = sbuf("warm", [P, 1], F32)
        ident = sbuf("ident", [P, P], F32)
        ident_bf = sbuf("ident_bf", [P, P], BF16)
        neg_mix = sbuf("neg_mix", [P, 2], F32)
        diag = sbuf("diag", [P, P], BF16)
        scale_bc = sbuf("scale_bc", [P, D], F32)

        def operand(name, count):
            return [
                (
                    sbuf("%s_grouped%d" % (name, i), [P, 512, T], BF16),
                    sbuf("%s_codes%d" % (name, i), [P, 512], U32),
                    sbuf("%s_scales%d" % (name, i), [P, 512], U8),
                )
                for i in range(count)
            ]

        x_op = operand("x", B)
        w_op = operand("w", 1)
        wv_op = operand("wv", 1)
        p_op = operand("p", B)
        v_op = operand("v", B)

        x_sb = per_batch("x_sb", [P, T, D], BF16)
        syn_t = per_tile("syn_t", [P, S], F32)
        neg_max = per_tile("neg_max", [P, 1], F32)
        e_sb = per_tile("e_sb", [P, S], F32)
        pc_sb = per_tile("pc_sb", [P, S], BF16)
        row_sum = per_batch("row_sum", [P, T], F32)
        inv_sum = per_batch("inv_sum", [P, T], F32)

        nc.scalar.dma_start(out=mix_bc[:], in_=mix.partition_broadcast(P))
        nc.scalar.dma_start(out=u4[:], in_=u.rearrange("(p t) -> p t", t=T))
        nc.sync.dma_start(out=scale4[:], in_=x_scale.rearrange("a b (p j) -> p (a b j)", j=T))

        def load_half(tiles, matrix, h):
            nc.sync.dma_start(out=tiles[h][:], in_=matrix.rearrange("(p j) n -> p j n", j=T)[:, :, h * H : (h + 1) * H])

        def load_x(b):
            nc.sync.dma_start(out=x_raw[b][:], in_=x_bytes[b].rearrange("(p t) k -> p t k", t=T))

        load_half(w_raw, w, 0)
        load_x(0)
        load_half(w_raw, w, 1)
        load_x(1)
        load_half(wv_raw, wv, 0)
        load_half(wv_raw, wv, 1)
        nc.sync.dma_start(out=rnd_sb[:], in_=rnd.rearrange("(p t) k -> p t k", t=T))
        nc.sync.dma_start(out=c_bc[:], in_=c.partition_broadcast(P))

        nc.vector.memset(warm[:], 0.0)
        nc.scalar.activation(out=warm[:], in_=warm[:], func=ACT.Exp)
        make_identity(nc, ident[:])
        make_identity(nc, ident_bf[:])
        nc.gpsimd.tensor_scalar(out=neg_mix[:], in0=mix_bc[:], scalar1=-1.0, scalar2=0.0, op0=MULT, op1=ADD)
        nc.gpsimd.tensor_scalar(out=diag[:], in0=ident_bf[:], scalar1=neg_mix[:, 1:2], scalar2=0.0, op0=MULT, op1=ADD)

        banks = {}

        def new_bank(pool, key):
            banks[key] = pool.tile([P, BANK], F32, name="bank", tag="bank")
            return banks[key]

        def quantise(op, lo, hi):
            grouped, codes, scales = op
            nc.vector.quantize_mx(
                out=codes[:, lo:hi].bitcast(FP8X4),
                scales=scales[:, lo:hi],
                in_=grouped[:, lo:hi, :].rearrange("p n j -> p (n j)"),
            )

        def multiply(out_ap, lhs, lhs_cols, rhs, rhs_cols):
            nc.tensor.matmul_mx(
                out=out_ap,
                lhsT=lhs[1][:, lhs_cols].bitcast(FP8X4),
                lhsT_scale=lhs[2][:, lhs_cols],
                rhs=rhs[1][:, rhs_cols].bitcast(FP8X4),
                rhs_scale=rhs[2][:, rhs_cols],
                start=True,
                stop=True,
            )

        def weave(copy, op, raw, h):
            copy(
                out=op[0][:, h * H : (h + 1) * H, :].rearrange("p (n i) j -> p n j i", i=4),
                in_=raw[h][:].rearrange("p j (n i) -> p n j i", i=4),
            )

        def turn(bank, at, words):
            nc.tensor.transpose(bank[:, blk(at)], words, ident[:])

        def unload_words(bank, op, tile, tiles):
            grouped = op[0][:, tile * P : (tile + tiles) * P, :].rearrange("p r j -> p (r j)").bitcast(F32)
            nc.scalar.copy(
                out=grouped.rearrange("p (t r h) -> p t r h", t=tiles, h=2),
                in_=bank[:, : tiles * 2 * P].rearrange("p (t h r) -> p t r h", t=tiles, h=2),
            )

        idle = new_bank(ps_turn, "idle")
        for i in range(5):
            nc.tensor.matmul(idle[:, blk(i % T)], lhsT=ident[:], rhs=ident[:], start=True, stop=True)

        def turn_scale(i):
            bank = new_bank(ps_turn, "scale")
            for j in range(T):
                turn(bank, j, scale4[:, j : j + 1].to_broadcast([P, P]))

        def spread_scale(i):
            nc.scalar.copy(
                out=scale_bc[:].rearrange("p (q j) -> p q j", j=T), in_=banks["scale"][:].rearrange("p (j q) -> p q j", j=T)
            )

        def weave_w(h):
            weave(nc.scalar.copy if h else nc.vector.tensor_copy, w_op[0], w_raw, h)

        def quantise_w(i):
            quantise(w_op[0], 0, S)

        def weave_wv(h):
            weave(nc.scalar.copy, wv_op[0], wv_raw, h)

        def quantise_wv(i):
            quantise(wv_op[0], 0, D)

        def widen(i):
            b, t = divmod(i, T)
            nc.vector.tensor_tensor(out=x_sb[b][:, t, :], in0=x_raw[b][:, t, :].bitcast(FP8), in1=scale_bc[:], op=MULT)

        def turn_x(i):
            b, pair = divmod(i, 2)
            bank = new_bank(ps_turn, ("x", i))
            for t in range(2):
                words = x_sb[b][:, 2 * pair + t, :].bitcast(F32)
                for h in range(2):
                    turn(bank, 2 * t + h, words[:, h::2])

        def unload_x(i):
            b, pair = divmod(i, 2)
            unload_words(banks[("x", i)], x_op[b], 2 * pair, 2)

        def quantise_x(b):
            quantise(x_op[b], 0, S)

        def score(i):
            b, kb = divmod(i, T)
            multiply(new_bank(ps_mx, ("score", i))[:], w_op[0], blk(kb), x_op[b], slice(0, S))

        def unload_score(i):
            b, kb = divmod(i, T)
            nc.scalar.activation(out=syn_t[b][kb][:], in_=banks[("score", i)][:], func=ACT.Copy, scale=neg_mix[:, 0:1])

        def add_rnd(i):
            bank = new_bank(ps_logit, ("logit", i))
            nc.tensor.matmul(bank[:], lhsT=diag[:], rhs=rnd_sb[:, i % T, :], start=True, stop=False)

        def add_score(i):
            b, t = divmod(i, T)
            for kb in range(T):
                nc.tensor.matmul(
                    banks[("logit", i)][:, blk(kb)],
                    lhsT=syn_t[b][kb][:, blk(t)],
                    rhs=ident[:],
                    start=False,
                    stop=(kb == T - 1),
                    is_transpose=True,
                )

        def reorder_c(i):
            nc.scalar.copy(
                out=c_split[:].rearrange("p (h q e) -> p h q e", h=2, e=2), in_=c_bc[:].rearrange("p (q h e) -> p h q e", h=2, e=2)
            )

        def row_max(i):
            b, t = divmod(i, T)
            nc.vector.tensor_reduce(out=neg_max[b][t][:], in_=banks[("logit", i)][:], axis=AX.X, op=MIN)

        def exp(i):
            b, t = divmod(i, T)
            nc.scalar.activation(
                out=e_sb[b][t][:].rearrange("p (h q e) -> p h q e", h=2, e=2),
                in_=banks[("logit", i)][:].rearrange("p (q h e) -> p h q e", h=2, e=2),
                func=ACT.Exp,
                bias=neg_max[b][t][:],
                scale=-1.0,
                accum_out=row_sum[b][:, t : t + 1],
            )

        def reciprocal(i):
            b, pair = divmod(i, 2)
            cols = slice(2 * pair, 2 * pair + 2)
            nc.vector.reciprocal(out=inv_sum[b][:, cols], in_=row_sum[b][:, cols])

        def probs(i):
            b, t = divmod(i, T)
            nc.vector.scalar_tensor_tensor(
                out=pc_sb[b][t][:], in0=e_sb[b][t][:], scalar=inv_sum[b][:, t : t + 1], in1=c_split[:], op0=MULT, op1=MULT
            )

        def turn_probs(i):
            b, t = divmod(i, T)
            bank = new_bank(ps_turn, ("probs", i))
            words = pc_sb[b][t][:].bitcast(F32)
            for h in range(2):
                turn(bank, h, words[:, blk(h)])

        def unload_probs(i):
            b, t = divmod(i, T)
            unload_words(banks[("probs", i)], p_op[b], t, 1)

        quantise_probs_tiles = [(0, 0, 2), (0, 2, 4)] + [(1, t, t + 1) for t in range(T)]

        def quantise_probs(i):
            b, first, end = quantise_probs_tiles[i]
            quantise(p_op[b], first * P, end * P)

        def value(i):
            b, fb = divmod(i, T)
            bank = new_bank(ps_mx, ("value", i))
            for t in range(T):
                multiply(bank[:, blk(t)], x_op[b], blk(t), wv_op[0], blk(fb))

        def unload_value(i):
            b, fb = divmod(i, T)
            nc.vector.tensor_tensor(
                out=v_op[b][0][:, blk(fb), :],
                in0=banks[("value", i)][:].rearrange("p (t n) -> p n t", t=T),
                in1=u4[:].unsqueeze(1).to_broadcast([P, P, T]),
                op=MULT,
            )

        def quantise_value(b):
            quantise(v_op[b], 0, D)

        result_parts = [(b, t, 0, D) for b in range(B) for t in range(T)][:-1] + [(B - 1, T - 1, 0, H), (B - 1, T - 1, H, D)]
        vector_parts = (5, 7,)

        def result(i):
            b, t, lo, hi = result_parts[i]
            multiply(new_bank(ps_mx, ("result", i))[:, : hi - lo], p_op[b], blk(t), v_op[b], slice(lo, hi))

        def store(i):
            b, t, lo, hi = result_parts[i]
            o_sb = stage_out.tile([P, D], F32, name="o_sb")
            copy = nc.vector.tensor_copy if i in vector_parts else nc.scalar.copy
            copy(out=o_sb[:, : hi - lo], in_=banks[("result", i)][:, : hi - lo])
            nc.sync.dma_start(out=out[b].rearrange("(p t) f -> p t f", t=T)[:, t, lo:hi], in_=o_sb[:, : hi - lo])

        stages = {
            "turn_scale": turn_scale,
            "spread_scale": spread_scale,
            "weave_w": weave_w,
            "quantise_w": quantise_w,
            "weave_wv": weave_wv,
            "quantise_wv": quantise_wv,
            "widen": widen,
            "turn_x": turn_x,
            "unload_x": unload_x,
            "quantise_x": quantise_x,
            "score": score,
            "unload_score": unload_score,
            "add_rnd": add_rnd,
            "add_score": add_score,
            "reorder_c": reorder_c,
            "row_max": row_max,
            "exp": exp,
            "reciprocal": reciprocal,
            "probs": probs,
            "turn_probs": turn_probs,
            "unload_probs": unload_probs,
            "quantise_probs": quantise_probs,
            "value": value,
            "unload_value": unload_value,
            "quantise_value": quantise_value,
            "result": result,
            "store": store,
        }
        items = {}
        for name in ORDER.split():
            item = items.get(name, 0)
            items[name] = item + 1
            stages[name](item)
